import numpy as np
import ml_dtypes


def mxq(x, axis, fmt="e4m3"):
    dtype, down = {"e4m3": (ml_dtypes.float8_e4m3fn, 7), "e5m2": (ml_dtypes.float8_e5m2, 14)}[fmt]
    v = np.moveaxis(np.asarray(x, np.float32).astype(ml_dtypes.bfloat16).astype(np.float64), axis, -1)
    blocks = v.reshape(v.shape[:-1] + (-1, 32))
    amax = np.abs(blocks).max(-1, keepdims=True)
    byte = np.maximum(np.where(amax > 0, np.frexp(amax)[1] - 1 + 127, 0) - down, 1)
    scale = np.exp2(byte - 127.0)
    codes = (blocks / scale).astype(np.float32).astype(dtype).astype(np.float64)
    return np.moveaxis((codes * scale).reshape(v.shape), -1, axis)


WIDE = False


def mx_kscale(k):
    if not WIDE:
        return np.ones(k)
    levels = np.array([10, -10, 5, -5, 0])
    if k % 512:
        return np.exp2(np.random.permutation(np.resize(levels, k // 32))).repeat(32)
    a = np.empty((k // 512, 16))
    for p in range(k // 512):
        a[p, :8] = np.random.permutation(np.resize(levels, 8))
        for g in range(8):
            far = levels[np.abs(levels - a[p, g]) >= 10]
            a[p, g + 8] = far[np.random.randint(len(far))]
    return np.exp2(a.ravel()).repeat(32)


def f64(x):
    return np.asarray(x).astype(np.float64)


def striped8(idx):
    return np.concatenate([v.reshape(-1, 16).T for v in idx]).astype(np.uint16)


def unstriped8(offs):
    return np.stack([offs[16 * g:16 * g + 16].T.reshape(-1) for g in range(8)]).astype(np.int64)


E2M1 = np.array([0.0, 0.5, 1.0, 1.5, 2.0, 3.0, 4.0, 6.0, -0.0, -0.5, -1.0, -1.5, -2.0, -3.0, -4.0, -6.0])


def pack_weight(w, fmt):
    k, n = w.shape
    w = f64(np.asarray(w, np.float32).astype(ml_dtypes.bfloat16)).reshape(k // 32, 32, n)
    amax = np.abs(w).max(1)
    if fmt == "e4m3":
        byte = np.frexp(amax)[1] - 1 + 127 - 7
    else:
        mant, ex = np.frexp(amax / 6.0)
        byte = np.where(mant > 0.5, ex, ex - 1) + 127
    byte = np.clip(np.where(amax > 0, byte, 1), 1, 254)
    scaled = (w * np.exp2(127.0 - byte)[:, None, :]).reshape(k, n).astype(np.float32)
    by_word = np.ascontiguousarray(scaled.reshape(k // 512, 128, 4, n).transpose(0, 1, 3, 2))
    if fmt == "e4m3":
        words = by_word.astype(ml_dtypes.float8_e4m3fn).view(np.uint8)
    else:
        c = by_word.astype(ml_dtypes.float4_e2m1fn).view(np.uint8) & 0xF
        words = (c[..., 0::2] | (c[..., 1::2] << 4)).reshape(k // 512, 128, 2 * n)
    return np.ascontiguousarray(words), np.ascontiguousarray(byte.astype(np.uint8).reshape(k // 512, 16, n))


def unpack_weight(words, scales, fmt):
    g, _, n = scales.shape
    words = np.ascontiguousarray(words).reshape(g, 128, n, -1)
    if fmt == "e4m3":
        vals = words.view(ml_dtypes.float8_e4m3fn).astype(np.float64)
    else:
        nib = np.empty((g, 128, n, 4), np.uint8)
        nib[..., 0::2] = words & 0xF
        nib[..., 1::2] = words >> 4
        vals = E2M1[nib]
    vals = vals * np.repeat(np.exp2(scales.astype(np.float64) - 127.0), 8, axis=1)[..., None]
    return vals.transpose(0, 1, 3, 2).reshape(g * 512, n)


K, M, T, S = 1536, 512, 2048, 512


def setup_inputs():
    n = np.random.standard_normal
    s = mx_kscale(K)[:, None]
    p_w = pack_weight(n((K, M)) / np.sqrt(K) / s, "e4m3")
    return {
        "xT": (n((K, T)) * s).astype(np.float32),
        "w_words": p_w[0],
        "w_scales": p_w[1],
        "wgt": np.repeat(np.random.uniform(0.5, 2.0, (8, S)), 16, axis=0).astype(np.float32),
        "offs": striped8(np.stack([np.random.permutation(T)[:S] for _ in range(8)])),
    }


def reference(xT, w_words, w_scales, wgt, offs):
    idx = unstriped8(offs)
    group = np.arange(K) % 512 // 64
    xg = f64(wgt)[np.arange(K) // 4 % 128] * f64(xT)[np.arange(K)[:, None], idx[group]]
    xT_ = mxq(xg, 0, "e4m3")
    w_ = unpack_weight(w_words, w_scales, "e4m3")
    y = w_.T @ xT_
    return y

@@ -1,0 +1,140 @@
+from contextlib import ExitStack
+
+import concourse.mybir as mybir
+
+K, M, T, S = 1536, 512, 2048, 512
+FLOPS = 2 * K * M * S
+
+F32 = mybir.dt.float32
+BF16 = mybir.dt.bfloat16
+I32 = mybir.dt.int32
+U8 = mybir.dt.uint8
+U16 = mybir.dt.uint16
+U32 = mybir.dt.uint32
+FP8X4 = mybir.dt.float8_e4m3fn_x4
+MULT = mybir.AluOpType.mult
+
+P = 128
+PASSES = K // (4 * P)
+HALF = S // 2
+LIST_COLS = HALF // 16
+MT = M // P
+
+
+def tile_list_heads_none_kernel(tc, xT, w_words, w_scales, wgt, offs, out):
+    nc = tc.nc
+    with ExitStack() as ctx:
+        keep = ctx.enter_context(tc.tile_pool(name="keep", bufs=1))
+        psum = ctx.enter_context(tc.psum_pool(name="psum", bufs=1))
+
+        offsets = keep.tile([P, S // 16], U16, name="offsets")
+        nc.sync.dma_start(offsets[:], offs)
+        wgt_sb = keep.tile([P, S], F32, name="wgt_sb")
+
+        w_planes = keep.tile([P, M], U8, name="w_planes", align_bytes=64)
+        nc.gpsimd.memset(w_planes[:].bitcast(I32), 0)
+        for q in range(4):
+            nc.scalar.dma_start(
+                w_planes[32 * q : 32 * q + 4 * PASSES, :].bitcast(I32),
+                w_scales[:, 4 * q : 4 * q + 4, :].bitcast(I32),
+            )
+
+        w_sb = [keep.tile([P, M], I32, name="w_sb%d" % a, align_bytes=64) for a in range(PASSES)]
+
+        def load_w(a):
+            nc.sync.dma_start(w_sb[a][:], w_words[a].rearrange("p n t -> p (n t)").bitcast(I32))
+
+        x_sb = {}
+        for a in range(PASSES):
+            rows = xT[4 * P * a : 4 * P * (a + 1), :].rearrange("(p t) c -> p t c", t=4)
+            for t in range(4):
+                x_sb[a, t] = keep.tile([P, T], F32, name="x%d%d" % (a, t))
+                nc.sync.dma_start(x_sb[a, t][:], rows[:, t, :])
+                if (a, t) == (0, 0):
+                    nc.sync.dma_start(wgt_sb[:], wgt)
+                if (a, t) == (1, 0):
+                    load_w(0)
+        load_w(1)
+        load_w(2)
+
+        g, xb, codes, scales = {}, {}, {}, {}
+        for a in range(PASSES):
+            for h in range(2):
+                g[a, h] = keep.tile([P, 4, HALF], F32, name="g%d%d" % (a, h))
+                xb[a, h] = keep.tile([P, HALF, 4], BF16, name="xb%d%d" % (a, h), align_bytes=64)
+                codes[a, h] = keep.tile([P, HALF], U32, name="codes%d%d" % (a, h), align_bytes=64)
+                scales[a, h] = keep.tile([P, HALF], U8, name="scales%d%d" % (a, h), align_bytes=64)
+        acc = {}
+        for h in range(2):
+            for m in range(MT):
+                acc[m, h] = psum.tile([P, HALF], F32, name="acc%d%d" % (m, h))
+
+        def gather(a, t, h):
+            nc.vector.tensor_tensor(
+                g[a, h][:, t, :],
+                x_sb[a, t][:].indirect(offsets[:, h * LIST_COLS : (h + 1) * LIST_COLS]),
+                wgt_sb[:, h * HALF : (h + 1) * HALF],
+                MULT,
+            )
+
+        def interleave(copy, a, h, t0, t1):
+            copy(xb[a, h][:, :, t0:t1], g[a, h][:, t0:t1, :].rearrange("p t n -> p n t"))
+
+        def quantize(a, h):
+            nc.vector.quantize_mx(
+                out=codes[a, h][:].bitcast(FP8X4),
+                scales=scales[a, h][:],
+                in_=xb[a, h][:].rearrange("p n t -> p (n t)"),
+            )
+
+        def multiply(a, h):
+            for m in range(MT):
+                cols = slice(m * P, (m + 1) * P)
+                nc.tensor.matmul_mx(
+                    out=acc[m, h][:],
+                    lhsT=w_sb[a][:, cols].bitcast(FP8X4),
+                    lhsT_scale=w_planes[4 * a : P, cols],
+                    rhs=codes[a, h][:].bitcast(FP8X4),
+                    rhs_scale=scales[a, h][:],
+                    start=(a == 0),
+                    stop=(a == PASSES - 1),
+                )
+
+        for a in range(PASSES):
+            last = a == PASSES - 1
+            for t in range(4):
+                for h in range(2):
+                    gather(a, t, h)
+                if t == 0 and a > 0:
+                    for h in range(2):
+                        quantize(a - 1, h)
+                        multiply(a - 1, h)
+                if last and t == 1:
+                    for h in range(2):
+                        interleave(nc.scalar.copy, a, h, 0, 2)
+            if last:
+                interleave(nc.scalar.copy, a, 0, 2, 4)
+                interleave(nc.vector.tensor_copy, a, 1, 2, 4)
+            else:
+                for h in range(2):
+                    interleave(nc.scalar.copy, a, h, 0, 4)
+
+        out_v = out.rearrange("(m p) j -> p m j", p=P)
+        res = [keep.tile([P, MT, HALF], F32, name="res%d" % h) for h in range(2)]
+        for h in range(2):
+            quantize(PASSES - 1, h)
+        for h in range(2):
+            multiply(PASSES - 1, h)
+        cols = slice(0, HALF)
+        for m in range(MT):
+            nc.scalar.copy(res[0][:, m, :], acc[m, 0][:])
+            if m % 2:
+                nc.sync.dma_start(out_v[:, m - 1 : m + 1, cols], res[0][:, m - 1 : m + 1, :])
+        cols = slice(HALF, S)
+        for m in range(MT):
+            if m % 2:
+                nc.scalar.copy(res[1][:, m, :], acc[m, 1][:])
+                nc.scalar.dma_start(out_v[:, m, cols], res[1][:, m, :])
+            else:
+                nc.vector.tensor_copy(res[1][:, m, :], acc[m, 1][:])
+                nc.sync.dma_start(out_v[:, m, cols], res[1][:, m, :])

@@ -28,13 +28,12 @@ def tile_list_heads_none_kernel(tc, xT, w_words, w_scales, wgt, offs, out):
         psum = ctx.enter_context(tc.psum_pool(name="psum", bufs=1))
 
         offsets = keep.tile([P, S // 16], U16, name="offsets")
-        nc.sync.dma_start(offsets[:], offs)
         wgt_sb = keep.tile([P, S], F32, name="wgt_sb")
 
         w_planes = keep.tile([P, M], U8, name="w_planes", align_bytes=64)
         nc.gpsimd.memset(w_planes[:].bitcast(I32), 0)
         for q in range(4):
-            nc.scalar.dma_start(
+            nc.gpsimd.dma_start(
                 w_planes[32 * q : 32 * q + 4 * PASSES, :].bitcast(I32),
                 w_scales[:, 4 * q : 4 * q + 4, :].bitcast(I32),
             )
@@ -49,11 +48,12 @@ def tile_list_heads_none_kernel(tc, xT, w_words, w_scales, wgt, offs, out):
             rows = xT[4 * P * a : 4 * P * (a + 1), :].rearrange("(p t) c -> p t c", t=4)
             for t in range(4):
                 x_sb[a, t] = keep.tile([P, T], F32, name="x%d%d" % (a, t))
+                if (a, t) == (2, 3):
+                    load_w(0)
                 nc.sync.dma_start(x_sb[a, t][:], rows[:, t, :])
                 if (a, t) == (0, 0):
+                    nc.sync.dma_start(offsets[:], offs)
                     nc.sync.dma_start(wgt_sb[:], wgt)
-                if (a, t) == (1, 0):
-                    load_w(0)
         load_w(1)
         load_w(2)
 
@@ -77,8 +77,8 @@ def tile_list_heads_none_kernel(tc, xT, w_words, w_scales, wgt, offs, out):
                 MULT,
             )
 
-        def interleave(copy, a, h, t0, t1):
-            copy(xb[a, h][:, :, t0:t1], g[a, h][:, t0:t1, :].rearrange("p t n -> p n t"))
+        def interleave(copy, a, h, t0, t1, c0=0, c1=HALF):
+            copy(xb[a, h][:, c0:c1, t0:t1], g[a, h][:, t0:t1, c0:c1].rearrange("p t n -> p n t"))
 
         def quantize(a, h):
             nc.vector.quantize_mx(
@@ -114,7 +114,8 @@ def tile_list_heads_none_kernel(tc, xT, w_words, w_scales, wgt, offs, out):
                         interleave(nc.scalar.copy, a, h, 0, 2)
             if last:
                 interleave(nc.scalar.copy, a, 0, 2, 4)
-                interleave(nc.vector.tensor_copy, a, 1, 2, 4)
+                interleave(nc.scalar.copy, a, 1, 2, 4, 0, HALF // 2)
+                interleave(nc.vector.tensor_copy, a, 1, 2, 4, HALF // 2, HALF)
             else:
                 for h in range(2):
                     interleave(nc.scalar.copy, a, h, 0, 4)

@@ -28,7 +28,17 @@ def tile_list_heads_none_kernel(tc, xT, w_words, w_scales, wgt, offs, out):
         psum = ctx.enter_context(tc.psum_pool(name="psum", bufs=1))
 
         offsets = keep.tile([P, S // 16], U16, name="offsets")
-        wgt_sb = keep.tile([P, S], F32, name="wgt_sb")
+        wgt_sb = keep.tile([P, S], F32, name="wgt_sb", align_bytes=64)
+        wgt_rows = keep.tile([P, 32], F32, name="wgt_rows", align_bytes=64)
+        wgt_cols = keep.tile([P, 32], F32, name="wgt_cols", align_bytes=64)
+        wgt_spread = keep.tile([P, S], F32, name="wgt_spread", align_bytes=64)
+        nc.scalar.dma_start(wgt_rows[:], wgt.rearrange("(g r) (b q) -> g r b q", r=16, q=32)[:, 0, :, :])
+        nc.vector.transpose(wgt_cols[:], wgt_rows[:])
+        nc.vector.tensor_copy(
+            wgt_spread[:].rearrange("p (b e r) -> p b e r", e=2, r=16),
+            wgt_cols[:].rearrange("p (e b) -> p b e", e=2).unsqueeze(3).to_broadcast([P, S // 32, 2, 16]),
+        )
+        nc.vector.transpose(wgt_sb[:], wgt_spread[:])
 
         w_planes = keep.tile([P, M], U8, name="w_planes", align_bytes=64)
         nc.gpsimd.memset(w_planes[:].bitcast(I32), 0)
@@ -53,7 +63,6 @@ def tile_list_heads_none_kernel(tc, xT, w_words, w_scales, wgt, offs, out):
                 nc.sync.dma_start(x_sb[a, t][:], rows[:, t, :])
                 if (a, t) == (0, 0):
                     nc.sync.dma_start(offsets[:], offs)
-                    nc.sync.dma_start(wgt_sb[:], wgt)
         load_w(1)
         load_w(2)
 
@@ -69,11 +78,12 @@ def tile_list_heads_none_kernel(tc, xT, w_words, w_scales, wgt, offs, out):
             for m in range(MT):
                 acc[m, h] = psum.tile([P, HALF], F32, name="acc%d%d" % (m, h))
 
-        def gather(a, t, h):
+        def gather(a, t, h, c0=0, c1=HALF):
+            j0, j1 = h * HALF + c0, h * HALF + c1
             nc.vector.tensor_tensor(
-                g[a, h][:, t, :],
-                x_sb[a, t][:].indirect(offsets[:, h * LIST_COLS : (h + 1) * LIST_COLS]),
-                wgt_sb[:, h * HALF : (h + 1) * HALF],
+                g[a, h][:, t, c0:c1],
+                x_sb[a, t][:].indirect(offsets[:, j0 // 16 : j1 // 16]),
+                wgt_sb[:, j0:j1],
                 MULT,
             )
 
@@ -100,42 +110,42 @@ def tile_list_heads_none_kernel(tc, xT, w_words, w_scales, wgt, offs, out):
                     stop=(a == PASSES - 1),
                 )
 
+        last = PASSES - 1
         for a in range(PASSES):
-            last = a == PASSES - 1
-            for t in range(4):
+            for t in range(3 if a == last else 4):
                 for h in range(2):
                     gather(a, t, h)
                 if t == 0 and a > 0:
                     for h in range(2):
                         quantize(a - 1, h)
                         multiply(a - 1, h)
-                if last and t == 1:
+                if a == last and t == 1:
                     for h in range(2):
                         interleave(nc.scalar.copy, a, h, 0, 2)
-            if last:
-                interleave(nc.scalar.copy, a, 0, 2, 4)
-                interleave(nc.scalar.copy, a, 1, 2, 4, 0, HALF // 2)
-                interleave(nc.vector.tensor_copy, a, 1, 2, 4, HALF // 2, HALF)
-            else:
+            if a < last:
                 for h in range(2):
                     interleave(nc.scalar.copy, a, h, 0, 4)
 
         out_v = out.rearrange("(m p) j -> p m j", p=P)
         res = [keep.tile([P, MT, HALF], F32, name="res%d" % h) for h in range(2)]
+        mid = HALF // 2
+        gather(last, 3, 0)
+        gather(last, 3, 1, 0, mid)
+        interleave(nc.scalar.copy, last, 0, 2, 4, 0, mid)
+        interleave(nc.scalar.copy, last, 1, 2, 4, 0, mid)
+        interleave(nc.vector.tensor_copy, last, 0, 2, 4, mid, HALF)
+        quantize(last, 0)
+        multiply(last, 0)
+        gather(last, 3, 1, mid, HALF)
+        interleave(nc.vector.tensor_copy, last, 1, 2, 4, mid, HALF)
+        quantize(last, 1)
+        multiply(last, 1)
         for h in range(2):
-            quantize(PASSES - 1, h)
-        for h in range(2):
-            multiply(PASSES - 1, h)
-        cols = slice(0, HALF)
-        for m in range(MT):
-            nc.scalar.copy(res[0][:, m, :], acc[m, 0][:])
-            if m % 2:
-                nc.sync.dma_start(out_v[:, m - 1 : m + 1, cols], res[0][:, m - 1 : m + 1, :])
-        cols = slice(HALF, S)
-        for m in range(MT):
-            if m % 2:
-                nc.scalar.copy(res[1][:, m, :], acc[m, 1][:])
-                nc.scalar.dma_start(out_v[:, m, cols], res[1][:, m, :])
-            else:
-                nc.vector.tensor_copy(res[1][:, m, :], acc[m, 1][:])
-                nc.sync.dma_start(out_v[:, m, cols], res[1][:, m, :])
+            cols = slice(h * HALF, (h + 1) * HALF)
+            for m in range(MT):
+                if h == 1 and m % 2 == 0:
+                    nc.vector.tensor_copy(res[h][:, m, :], acc[m, h][:])
+                else:
+                    nc.scalar.copy(res[h][:, m, :], acc[m, h][:])
+                queue = nc.scalar if h == 1 and m % 2 else nc.sync
+                queue.dma_start(out_v[:, m, cols], res[h][:, m, :])

@@ -48,7 +48,7 @@ def tile_list_heads_none_kernel(tc, xT, w_words, w_scales, wgt, offs, out):
                 w_scales[:, 4 * q : 4 * q + 4, :].bitcast(I32),
             )
 
-        w_sb = [keep.tile([P, M], I32, name="w_sb%d" % a, align_bytes=64) for a in range(PASSES)]
+        w_sb = [keep.tile([P, M], I32, name="w_sb%d" % a, align_bytes=256) for a in range(PASSES)]
 
         def load_w(a):
             nc.sync.dma_start(w_sb[a][:], w_words[a].rearrange("p n t -> p (n t)").bitcast(I32))
@@ -57,7 +57,7 @@ def tile_list_heads_none_kernel(tc, xT, w_words, w_scales, wgt, offs, out):
         for a in range(PASSES):
             rows = xT[4 * P * a : 4 * P * (a + 1), :].rearrange("(p t) c -> p t c", t=4)
             for t in range(4):
-                x_sb[a, t] = keep.tile([P, T], F32, name="x%d%d" % (a, t))
+                x_sb[a, t] = keep.tile([P, T], F32, name="x%d%d" % (a, t), align_bytes=256)
                 if (a, t) == (2, 3):
                     load_w(0)
                 nc.sync.dma_start(x_sb[a, t][:], rows[:, t, :])
@@ -127,11 +127,12 @@ def tile_list_heads_none_kernel(tc, xT, w_words, w_scales, wgt, offs, out):
                     interleave(nc.scalar.copy, a, h, 0, 4)
 
         out_v = out.rearrange("(m p) j -> p m j", p=P)
-        res = [keep.tile([P, MT, HALF], F32, name="res%d" % h) for h in range(2)]
+        res = [keep.tile([P, MT, HALF], F32, name="res%d" % h, align_bytes=256) for h in range(2)]
         mid = HALF // 2
-        gather(last, 3, 0)
-        gather(last, 3, 1, 0, mid)
+        gather(last, 3, 0, 0, mid)
         interleave(nc.scalar.copy, last, 0, 2, 4, 0, mid)
+        gather(last, 3, 0, mid, HALF)
+        gather(last, 3, 1, 0, mid)
         interleave(nc.scalar.copy, last, 1, 2, 4, 0, mid)
         interleave(nc.vector.tensor_copy, last, 0, 2, 4, mid, HALF)
         quantize(last, 0)
@@ -147,5 +148,4 @@ def tile_list_heads_none_kernel(tc, xT, w_words, w_scales, wgt, offs, out):
                     nc.vector.tensor_copy(res[h][:, m, :], acc[m, h][:])
                 else:
                     nc.scalar.copy(res[h][:, m, :], acc[m, h][:])
-                queue = nc.scalar if h == 1 and m % 2 else nc.sync
-                queue.dma_start(out_v[:, m, cols], res[h][:, m, :])
+                nc.sync.dma_start(out_v[:, m, cols], res[h][:, m, :])

from contextlib import ExitStack

import concourse.mybir as mybir

K, M, T, S = 1536, 512, 2048, 512
FLOPS = 2 * K * M * S

F32 = mybir.dt.float32
BF16 = mybir.dt.bfloat16
I32 = mybir.dt.int32
U8 = mybir.dt.uint8
U16 = mybir.dt.uint16
U32 = mybir.dt.uint32
FP8X4 = mybir.dt.float8_e4m3fn_x4
MULT = mybir.AluOpType.mult

P = 128
PASSES = K // (4 * P)
HALF = S // 2
LIST_COLS = HALF // 16
MT = M // P


def tile_list_heads_none_kernel(tc, xT, w_words, w_scales, wgt, offs, out):
    nc = tc.nc
    with ExitStack() as ctx:
        keep = ctx.enter_context(tc.tile_pool(name="keep", bufs=1))
        psum = ctx.enter_context(tc.psum_pool(name="psum", bufs=1))

        offsets = keep.tile([P, S // 16], U16, name="offsets")
        wgt_sb = keep.tile([P, S], F32, name="wgt_sb", align_bytes=64)
        wgt_rows = keep.tile([P, 32], F32, name="wgt_rows", align_bytes=64)
        wgt_cols = keep.tile([P, 32], F32, name="wgt_cols", align_bytes=64)
        wgt_spread = keep.tile([P, S], F32, name="wgt_spread", align_bytes=64)
        nc.scalar.dma_start(wgt_rows[:], wgt.rearrange("(g r) (b q) -> g r b q", r=16, q=32)[:, 0, :, :])
        nc.vector.transpose(wgt_cols[:], wgt_rows[:])
        nc.vector.tensor_copy(
            wgt_spread[:].rearrange("p (b e r) -> p b e r", e=2, r=16),
            wgt_cols[:].rearrange("p (e b) -> p b e", e=2).unsqueeze(3).to_broadcast([P, S // 32, 2, 16]),
        )
        nc.vector.transpose(wgt_sb[:], wgt_spread[:])

        w_planes = keep.tile([P, M], U8, name="w_planes", align_bytes=64)
        nc.gpsimd.memset(w_planes[:].bitcast(I32), 0)
        for q in range(4):
            nc.gpsimd.dma_start(
                w_planes[32 * q : 32 * q + 4 * PASSES, :].bitcast(I32),
                w_scales[:, 4 * q : 4 * q + 4, :].bitcast(I32),
            )

        w_sb = [keep.tile([P, M], I32, name="w_sb%d" % a, align_bytes=256) for a in range(PASSES)]

        def load_w(a):
            nc.sync.dma_start(w_sb[a][:], w_words[a].rearrange("p n t -> p (n t)").bitcast(I32))

        x_sb = {}
        for a in range(PASSES):
            rows = xT[4 * P * a : 4 * P * (a + 1), :].rearrange("(p t) c -> p t c", t=4)
            for t in range(4):
                x_sb[a, t] = keep.tile([P, T], F32, name="x%d%d" % (a, t), align_bytes=256)
                if (a, t) == (2, 3):
                    load_w(0)
                nc.sync.dma_start(x_sb[a, t][:], rows[:, t, :])
                if (a, t) == (0, 0):
                    nc.sync.dma_start(offsets[:], offs)
        load_w(1)
        load_w(2)

        g, xb, codes, scales = {}, {}, {}, {}
        for a in range(PASSES):
            for h in range(2):
                g[a, h] = keep.tile([P, 4, HALF], F32, name="g%d%d" % (a, h))
                xb[a, h] = keep.tile([P, HALF, 4], BF16, name="xb%d%d" % (a, h), align_bytes=64)
                codes[a, h] = keep.tile([P, HALF], U32, name="codes%d%d" % (a, h), align_bytes=64)
                scales[a, h] = keep.tile([P, HALF], U8, name="scales%d%d" % (a, h), align_bytes=64)
        acc = {}
        for h in range(2):
            for m in range(MT):
                acc[m, h] = psum.tile([P, HALF], F32, name="acc%d%d" % (m, h))

        def gather(a, t, h, c0=0, c1=HALF):
            j0, j1 = h * HALF + c0, h * HALF + c1
            nc.vector.tensor_tensor(
                g[a, h][:, t, c0:c1],
                x_sb[a, t][:].indirect(offsets[:, j0 // 16 : j1 // 16]),
                wgt_sb[:, j0:j1],
                MULT,
            )

        def interleave(copy, a, h, t0, t1, c0=0, c1=HALF):
            copy(xb[a, h][:, c0:c1, t0:t1], g[a, h][:, t0:t1, c0:c1].rearrange("p t n -> p n t"))

        def quantize(a, h):
            nc.vector.quantize_mx(
                out=codes[a, h][:].bitcast(FP8X4),
                scales=scales[a, h][:],
                in_=xb[a, h][:].rearrange("p n t -> p (n t)"),
            )

        def multiply(a, h):
            for m in range(MT):
                cols = slice(m * P, (m + 1) * P)
                nc.tensor.matmul_mx(
                    out=acc[m, h][:],
                    lhsT=w_sb[a][:, cols].bitcast(FP8X4),
                    lhsT_scale=w_planes[4 * a : P, cols],
                    rhs=codes[a, h][:].bitcast(FP8X4),
                    rhs_scale=scales[a, h][:],
                    start=(a == 0),
                    stop=(a == PASSES - 1),
                )

        last = PASSES - 1
        for a in range(PASSES):
            for t in range(3 if a == last else 4):
                for h in range(2):
                    gather(a, t, h)
                if t == 0 and a > 0:
                    for h in range(2):
                        quantize(a - 1, h)
                        multiply(a - 1, h)
                if a == last and t == 1:
                    for h in range(2):
                        interleave(nc.scalar.copy, a, h, 0, 2)
            if a < last:
                for h in range(2):
                    interleave(nc.scalar.copy, a, h, 0, 4)

        out_v = out.rearrange("(m p) j -> p m j", p=P)
        res = [keep.tile([P, MT, HALF], F32, name="res%d" % h, align_bytes=256) for h in range(2)]
        mid = HALF // 2
        gather(last, 3, 0, 0, mid)
        interleave(nc.scalar.copy, last, 0, 2, 4, 0, mid)
        gather(last, 3, 0, mid, HALF)
        gather(last, 3, 1, 0, mid)
        interleave(nc.scalar.copy, last, 1, 2, 4, 0, mid)
        interleave(nc.vector.tensor_copy, last, 0, 2, 4, mid, HALF)
        quantize(last, 0)
        multiply(last, 0)
        gather(last, 3, 1, mid, HALF)
        interleave(nc.vector.tensor_copy, last, 1, 2, 4, mid, HALF)
        quantize(last, 1)
        multiply(last, 1)
        for h in range(2):
            cols = slice(h * HALF, (h + 1) * HALF)
            for m in range(MT):
                if h == 1 and m % 2 == 0:
                    nc.vector.tensor_copy(res[h][:, m, :], acc[m, h][:])
                else:
                    nc.scalar.copy(res[h][:, m, :], acc[m, h][:])
                nc.sync.dma_start(out_v[:, m, cols], res[h][:, m, :])
